import numpy as np
import ml_dtypes


def mxq(x, axis, fmt="e4m3"):
    dtype, down = {"e4m3": (ml_dtypes.float8_e4m3fn, 7), "e5m2": (ml_dtypes.float8_e5m2, 14)}[fmt]
    v = np.moveaxis(np.asarray(x, np.float32).astype(ml_dtypes.bfloat16).astype(np.float64), axis, -1)
    blocks = v.reshape(v.shape[:-1] + (-1, 32))
    amax = np.abs(blocks).max(-1, keepdims=True)
    byte = np.maximum(np.where(amax > 0, np.frexp(amax)[1] - 1 + 127, 0) - down, 1)
    scale = np.exp2(byte - 127.0)
    codes = (blocks / scale).astype(np.float32).astype(dtype).astype(np.float64)
    return np.moveaxis((codes * scale).reshape(v.shape), -1, axis)


WIDE = False


def mx_kscale(k):
    if not WIDE:
        return np.ones(k)
    levels = np.array([10, -10, 5, -5, 0])
    if k % 512:
        return np.exp2(np.random.permutation(np.resize(levels, k // 32))).repeat(32)
    a = np.empty((k // 512, 16))
    for p in range(k // 512):
        a[p, :8] = np.random.permutation(np.resize(levels, 8))
        for g in range(8):
            far = levels[np.abs(levels - a[p, g]) >= 10]
            a[p, g + 8] = far[np.random.randint(len(far))]
    return np.exp2(a.ravel()).repeat(32)


def f64(x):
    return np.asarray(x).astype(np.float64)


def striped(idx):
    return np.tile(idx.reshape(-1, 16).T, (8, 1)).astype(np.uint16)


def unstriped(offs):
    return offs[:16].T.reshape(-1).astype(np.int64)


def pack_weight(w):
    k, n = w.shape
    w = f64(np.asarray(w, np.float32).astype(ml_dtypes.bfloat16)).reshape(k // 32, 32, n)
    amax = np.abs(w).max(1)
    byte = np.clip(np.where(amax > 0, np.frexp(amax)[1] - 1 + 127 - 7, 1), 1, 254)
    scaled = (w * np.exp2(127.0 - byte)[:, None, :]).reshape(k, n).astype(np.float32)
    words = np.ascontiguousarray(scaled.reshape(k // 512, 128, 4, n).transpose(0, 1, 3, 2)).astype(ml_dtypes.float8_e4m3fn).view(np.uint8)
    return words, np.ascontiguousarray(byte.astype(np.uint8).reshape(k // 512, 16, n))


def unpack_weight(words, scales):
    g, p, n, _ = words.shape
    vals = np.ascontiguousarray(words).view(ml_dtypes.float8_e4m3fn).astype(np.float64) * np.repeat(np.exp2(scales.astype(np.float64) - 127.0), 8, axis=1)[..., None]
    return vals.transpose(0, 1, 3, 2).reshape(g * 512, n)


E2M1 = np.array([0.0, 0.5, 1.0, 1.5, 2.0, 3.0, 4.0, 6.0, -0.0, -0.5, -1.0, -1.5, -2.0, -3.0, -4.0, -6.0])


def pack_fp4(w):
    k, n = w.shape
    w = f64(np.asarray(w, np.float32).astype(ml_dtypes.bfloat16)).reshape(k // 32, 32, n)
    amax = np.abs(w).max(1)
    mant, ex = np.frexp(amax / 6.0)
    byte = np.clip(np.where(amax > 0, np.where(mant > 0.5, ex, ex - 1) + 127, 1), 1, 254)
    scaled = (w * np.exp2(127.0 - byte)[:, None, :]).reshape(k, n).astype(np.float32)
    c = np.ascontiguousarray(scaled.reshape(k // 512, 128, 4, n).transpose(0, 1, 3, 2)).astype(ml_dtypes.float4_e2m1fn).view(np.uint8) & 0xF
    words = (c[..., 0::2] | (c[..., 1::2] << 4)).reshape(k // 512, 128, 2 * n)
    return np.ascontiguousarray(words), np.ascontiguousarray(byte.astype(np.uint8).reshape(k // 512, 16, n))


def unpack_fp4(words, scales):
    g, _, n = scales.shape
    words = np.ascontiguousarray(words).reshape(g, 128, n, 2)
    nib = np.empty((g, 128, n, 4), np.uint8)
    nib[..., 0::2] = words & 0xF
    nib[..., 1::2] = words >> 4
    vals = E2M1[nib] * np.repeat(np.exp2(scales.astype(np.float64) - 127.0), 8, axis=1)[..., None]
    return vals.transpose(0, 1, 3, 2).reshape(g * 512, n)


K, T, S, D, N, H, V, U = 512, 4096, 1024, 4, 128, 512, 256, 512


def setup_inputs():
    n = np.random.standard_normal
    s = mx_kscale(K)[:, None]
    u = mx_kscale(H)
    packed_xT = pack_weight(n((K, T)) * s)
    packed_w1 = pack_fp4(n((K, H)) / np.sqrt(K) / s)
    packed_w2 = pack_fp4(n((K, H)) / np.sqrt(K) / s)
    packed_w3 = pack_fp4(n((H, N)) / np.sqrt(H) / u[:, None])
    return {
        "x_words": packed_xT[0],
        "x_scales": packed_xT[1],
        "w1_words": packed_w1[0],
        "w1_scales": packed_w1[1],
        "w2_words": packed_w2[0],
        "w2_scales": packed_w2[1],
        "unit": (np.random.uniform(0.6, 1.4, (H, 1)) * u[:, None]).astype(np.float32),
        "w3_words": packed_w3[0],
        "w3_scales": packed_w3[1],
        "offs": striped(np.random.permutation(T)[:S]),
        "rdr": striped(np.random.permutation(np.concatenate([np.arange(V), np.random.randint(0, V, U - V)]))),
    }


def reference(x_words, x_scales, w1_words, w1_scales, w2_words, w2_scales, unit, w3_words, w3_scales, offs, rdr):
    xq = unpack_weight(x_words, x_scales)[:, unstriped(offs)]
    y = unpack_fp4(w1_words, w1_scales).T @ xq
    ay = np.abs(y)
    scl = ay.reshape(len(ay), -1, D).max(axis=2) + 0.2
    lev = y / np.repeat(scl, D, axis=1)
    yz = unpack_fp4(w2_words, w2_scales).T @ xq
    zero = yz.reshape(len(yz), -1, D).mean(axis=2)
    lz = lev * np.repeat(zero, D, axis=1)
    dq = lz.reshape(len(lz), -1, D).sum(axis=2)
    dr = dq[:, unstriped(rdr)]
    hid = f64(unit) * (dr * (np.tanh(zero[:, unstriped(rdr)])))
    return unpack_fp4(w3_words, w3_scales).T @ mxq(hid, 0, "e4m3")

@@ -1,0 +1,232 @@
+from contextlib import ExitStack
+
+import concourse.mybir as mybir
+
+F32 = mybir.dt.float32
+BF16 = mybir.dt.bfloat16
+I32 = mybir.dt.int32
+U32 = mybir.dt.uint32
+U16 = mybir.dt.uint16
+U8 = mybir.dt.uint8
+FP8X4 = mybir.dt.float8_e4m3fn_x4
+FP4X4 = mybir.dt.float4_e2m1fn_x4
+ACT = mybir.ActivationFunctionType
+ALU = mybir.AluOpType
+AX = mybir.AxisListType
+
+P = 128
+K, T, S, D, N, H, V, R = 512, 4096, 1024, 4, 128, 512, 256, 512
+PACK = 4
+HALVES = 2
+VH = V // HALVES
+SH = S // HALVES
+RH = R // HALVES
+FLOPS = 2 * K * H * S * 2 + 2 * H * N * R
+
+
+def load_scale_rows(queues, plane, rows):
+    for q in range(4):
+        queues[q].dma_start(out=plane[32 * q : 32 * q + 4, :].bitcast(I32), in_=rows[4 * q : 4 * q + 4, :].bitcast(I32))
+
+
+def tile_picked_ywvres_zero_p_kernel(tc, x_words, x_scales, w1_words, w1_scales, w2_words, w2_scales, unit, w3_words, w3_scales, offs, rdr, out):
+    nc = tc.nc
+    with ExitStack() as ctx:
+        keep = ctx.enter_context(tc.tile_pool(name="keep", bufs=1))
+        ybanks = ctx.enter_context(tc.psum_pool(name="ybanks", bufs=5))
+        fixed = ctx.enter_context(tc.psum_pool(name="fixed", bufs=1))
+
+        offs_sb = keep.tile([P, S // 16], U16, name="offs_sb")
+        rdr_sb = keep.tile([P, R // 16], U16, name="rdr_sb")
+        table_words = keep.tile([P, T], I32, name="table_words", align_bytes=64)
+        table_scales = keep.tile([P, T], U8, name="table_scales", align_bytes=64)
+        w_raw = [keep.tile([P, 2 * H], U8, name="w_raw%d" % j, align_bytes=64) for j in range(2)]
+        ws_raw = [keep.tile([P, H], U8, name="ws_raw%d" % j, align_bytes=64) for j in range(2)]
+
+        for j in range(2):
+            nc.gpsimd.memset(ws_raw[j][:].bitcast(I32), 0)
+        nc.vector.memset(table_scales[:].bitcast(I32), 0)
+
+        nc.sync.dma_start(offs_sb[:], offs)
+        nc.sync.dma_start(out=w_raw[0][:].bitcast(I32), in_=w1_words[0].bitcast(I32))
+        nc.sync.dma_start(rdr_sb[:], rdr)
+        nc.sync.dma_start(out=w_raw[1][:].bitcast(I32), in_=w2_words[0].bitcast(I32))
+        nc.sync.dma_start(out=table_words[:], in_=x_words[0].rearrange("p n t -> p (n t)").bitcast(I32))
+        load_scale_rows([nc.scalar] * 4, table_scales, x_scales[0])
+        load_scale_rows([nc.gpsimd] + [nc.scalar] * 3, ws_raw[0], w1_scales[0])
+        load_scale_rows([nc.gpsimd] * 4, ws_raw[1], w2_scales[0])
+
+        w_dealt = [keep.tile([P, PACK, 2 * P], U8, name="w_dealt%d" % j, align_bytes=64) for j in range(2)]
+        ws_dealt = [keep.tile([P, PACK, P], U8, name="ws_dealt%d" % j, align_bytes=64) for j in range(2)]
+
+        def deal_words(j):
+            nc.vector.tensor_copy(
+                out=w_dealt[j][:].rearrange("p t (m b) -> p t m b", b=2),
+                in_=w_raw[j][:].rearrange("p (m t b) -> p t m b", t=PACK, b=2),
+            )
+
+        def deal_scales(j):
+            nc.vector.tensor_copy(out=ws_dealt[j][:], in_=ws_raw[j][:].rearrange("p (m t) -> p t m", t=PACK))
+
+        picked_scales = keep.tile([P, S], U8, name="picked_scales", align_bytes=64)
+        x_scale = keep.tile([P, HALVES, D * VH], U8, name="x_scale", align_bytes=64)
+        x_code = [keep.tile([P, D * VH], U32, name="x_code%d" % h, align_bytes=64) for h in range(HALVES)]
+
+        deal_words(0)
+        deal_words(1)
+        nc.vector.tensor_copy(out=picked_scales[:], in_=table_scales[:].indirect(offs_sb[:]))
+        nc.vector.tensor_copy(
+            out=x_scale[:].rearrange("p h (d v) -> p h d v", d=D),
+            in_=picked_scales[:].rearrange("p (h v d) -> p h d v", h=HALVES, d=D),
+        )
+        deal_scales(0)
+        w3_sb = w_raw[0][:, 0 : 2 * N]
+        w3s_sb = ws_raw[0][:, 0:N]
+        unit_sb = keep.tile([P, PACK], F32, name="w_raw1", align_bytes=64)
+        nc.sync.dma_start(out=unit_sb[:], in_=unit.rearrange("(p t) o -> p (t o)", t=PACK))
+        nc.sync.dma_start(out=w3_sb.bitcast(I32), in_=w3_words[0].bitcast(I32))
+        load_scale_rows([nc.sync] * 4, w3s_sb, w3_scales[0])
+        for h in range(HALVES):
+            nc.vector.tensor_copy(
+                out=x_code[h][:].rearrange("p (d v) -> p v d", d=D),
+                in_=table_words[:].bitcast(U32).indirect(offs_sb[:, h * (SH // 16) : (h + 1) * (SH // 16)]),
+            )
+        deal_scales(1)
+
+        def product(dst, j, t, h, cols, start, stop):
+            nc.tensor.matmul_mx(
+                out=dst,
+                lhsT=w_dealt[j][:, t, :].bitcast(FP4X4),
+                lhsT_scale=ws_dealt[j][:, t, :],
+                rhs=x_code[h][:, cols].bitcast(FP8X4),
+                rhs_scale=x_scale[:, h, cols],
+                start=start,
+                stop=stop,
+            )
+
+        def group_sum(dst, j, t, h):
+            for d in range(D):
+                product(dst, j, t, h, slice(d * VH, (d + 1) * VH), d == 0, d == D - 1)
+
+        magnitude = [[keep.tile([P, 2, D * VH], F32, name="magnitude%d%d" % (h, tp)) for tp in range(2)] for h in range(HALVES)]
+        pair_max = [[keep.tile([P, 2, 2 * VH], F32, name="pair_max%d%d" % (h, tp)) for tp in range(2)] for h in range(HALVES)]
+        group_max = [keep.tile([P, 2, V], F32, name="group_max%d" % tp) for tp in range(2)]
+        y_sum_sb = keep.tile([P, 2, V], F32, name="y_sum_sb")
+        y_sum_ps = fixed.tile([P, 2, V], F32, name="y_sum_ps")
+        z_sum = [fixed.tile([P, PACK, VH], F32, name="z_sum%d" % h) for h in range(HALVES)]
+        z_tanh = [keep.tile([P, PACK, VH], F32, name="z_tanh%d" % h) for h in range(HALVES)]
+        z_term = keep.tile([P, HALVES, PACK, VH], F32, name="z_term")
+        window = [keep.tile([P, 4, V], F32, name="window%d" % t) for t in range(PACK)]
+        fetched = keep.tile([P, PACK, R], BF16, name="fetched", align_bytes=64)
+
+        def values(t, h):
+            y = ybanks.tile([P, D * VH], F32, name="y")
+            product(y[:], 0, t, h, slice(0, D * VH), True, True)
+            nc.scalar.activation(out=magnitude[h][t // 2][:, t % 2, :], in_=y[:], func=ACT.Abs)
+            if t < 2:
+                nc.vector.tensor_reduce(
+                    out=y_sum_sb[:, t, h * VH : (h + 1) * VH], in_=y[:].rearrange("p (d v) -> p v d", d=D), axis=AX.X, op=ALU.add
+                )
+
+        def first_max(h, tp):
+            mag = magnitude[h][tp]
+            nc.vector.tensor_tensor(out=pair_max[h][tp][:], in0=mag[:, :, 0 : 2 * VH], in1=mag[:, :, 2 * VH : 4 * VH], op=ALU.max)
+
+        def second_max(h, tp):
+            pm = pair_max[h][tp]
+            nc.vector.tensor_tensor(out=group_max[tp][:, :, h * VH : (h + 1) * VH], in0=pm[:, :, 0:VH], in1=pm[:, :, VH : 2 * VH], op=ALU.max)
+
+        def zero_points(h):
+            for t in range(PACK):
+                group_sum(z_sum[h][:, t, :], 1, t, h)
+            nc.scalar.activation(out=z_tanh[h][:], in_=z_sum[h][:], func=ACT.Tanh, scale=1.0 / D)
+
+        def zero_term(h):
+            nc.vector.scalar_tensor_tensor(
+                out=z_term[:, h, :, :], in0=z_sum[h][:], scalar=1.0 / D, in1=z_tanh[h][:], op0=ALU.mult, op1=ALU.mult
+            )
+
+        def inverse_scale(t):
+            nc.scalar.activation(out=window[t][:, 2, :], in_=group_max[t // 2][:, t % 2, :], func=ACT.Abs_reciprocal_sqrt, bias=0.2)
+            nc.scalar.activation(out=window[t][:, 3, :], in_=window[t][:, 2, :], func=ACT.Square)
+
+        def level_sum(t):
+            y_sum = y_sum_sb[:, t, :] if t < 2 else y_sum_ps[:, t - 2, :]
+            nc.vector.scalar_tensor_tensor(
+                out=window[t][:, 1, :], in0=y_sum, scalar=unit_sb[:, t : t + 1], in1=window[t][:, 3, :], op0=ALU.mult, op1=ALU.mult
+            )
+
+        def group_value(t):
+            nc.vector.tensor_tensor(
+                out=window[t][:, 0, :].rearrange("p (h v) -> p h v", h=HALVES),
+                in0=window[t][:, 1, :].rearrange("p (h v) -> p h v", h=HALVES),
+                in1=z_term[:, :, t, :],
+                op=ALU.mult,
+            )
+
+        def fetch(t, lo, hi, on_vector):
+            src = window[t][:].rearrange("p a v -> p (a v)").indirect(rdr_sb[:, lo // 16 : hi // 16])
+            if on_vector:
+                nc.vector.tensor_copy(out=fetched[:, t, lo:hi], in_=src)
+            else:
+                nc.scalar.activation(out=fetched[:, t, lo:hi], in_=src, func=ACT.Copy)
+
+        for t in range(PACK):
+            values(t, 0)
+        values(0, 1)
+        values(1, 1)
+        zero_points(0)
+        first_max(0, 0)
+        first_max(0, 1)
+        values(2, 1)
+        values(3, 1)
+        zero_points(1)
+        second_max(0, 0)
+        first_max(1, 0)
+        second_max(0, 1)
+        second_max(1, 0)
+        first_max(1, 1)
+        zero_term(0)
+        second_max(1, 1)
+        zero_term(1)
+        for t in (2, 3):
+            for h in range(HALVES):
+                group_sum(y_sum_ps[:, t - 2, h * VH : (h + 1) * VH], 0, t, h)
+        for t in range(PACK):
+            inverse_scale(t)
+        level_sum(0)
+        level_sum(1)
+        group_value(0)
+        group_value(1)
+        level_sum(2)
+        level_sum(3)
+        group_value(2)
+        group_value(3)
+        fetch(0, 0, RH, False)
+        fetch(1, 0, RH, False)
+        fetch(2, 0, RH, True)
+        fetch(3, 0, RH, True)
+        for t in range(PACK):
+            fetch(t, RH, R, False)
+
+        woven = [keep.tile([P, RH, PACK], BF16, name="woven%d" % c, align_bytes=64) for c in range(HALVES)]
+        hid_code = [keep.tile([P, RH], U32, name="hid_code%d" % c, align_bytes=64) for c in range(HALVES)]
+        hid_scale = [keep.tile([P, RH], U8, name="hid_scale%d" % c, align_bytes=64) for c in range(HALVES)]
+        for c in range(HALVES):
+            nc.vector.tensor_copy(out=woven[c][:], in_=fetched[:, :, c * RH : (c + 1) * RH].rearrange("p t r -> p r t"))
+        for c in range(HALVES):
+            nc.vector.quantize_mx(out=hid_code[c][:].bitcast(FP8X4), scales=hid_scale[c][:], in_=woven[c][:].rearrange("p r t -> p (r t)"))
+        for c in range(HALVES):
+            acc = ybanks.tile([P, D * VH], F32, name="y")
+            nc.tensor.matmul_mx(
+                out=acc[:, 0:RH],
+                lhsT=w3_sb.bitcast(FP4X4),
+                lhsT_scale=w3s_sb,
+                rhs=hid_code[c][:].bitcast(FP8X4),
+                rhs_scale=hid_scale[c][:],
+                start=True,
+                stop=True,
+            )
+            result = keep.tile([P, RH], F32, name="result%d" % c)
+            nc.scalar.copy(out=result[:], in_=acc[:, 0:RH])
+            nc.sync.dma_start(out=out[:, c * RH : (c + 1) * RH], in_=result[:])

@@ -43,18 +43,19 @@ def tile_picked_ywvres_zero_p_kernel(tc, x_words, x_scales, w1_words, w1_scales,
         w_raw = [keep.tile([P, 2 * H], U8, name="w_raw%d" % j, align_bytes=64) for j in range(2)]
         ws_raw = [keep.tile([P, H], U8, name="ws_raw%d" % j, align_bytes=64) for j in range(2)]
 
+        nc.gpsimd.memset(table_scales[:, 0 : T // 2].bitcast(I32), 0)
+        nc.vector.memset(table_scales[:, T // 2 : T].bitcast(I32), 0)
         for j in range(2):
             nc.gpsimd.memset(ws_raw[j][:].bitcast(I32), 0)
-        nc.vector.memset(table_scales[:].bitcast(I32), 0)
 
         nc.sync.dma_start(offs_sb[:], offs)
         nc.sync.dma_start(out=w_raw[0][:].bitcast(I32), in_=w1_words[0].bitcast(I32))
-        nc.sync.dma_start(rdr_sb[:], rdr)
         nc.sync.dma_start(out=w_raw[1][:].bitcast(I32), in_=w2_words[0].bitcast(I32))
+        load_scale_rows([nc.sync] * 4, table_scales, x_scales[0])
         nc.sync.dma_start(out=table_words[:], in_=x_words[0].rearrange("p n t -> p (n t)").bitcast(I32))
-        load_scale_rows([nc.scalar] * 4, table_scales, x_scales[0])
-        load_scale_rows([nc.gpsimd] + [nc.scalar] * 3, ws_raw[0], w1_scales[0])
-        load_scale_rows([nc.gpsimd] * 4, ws_raw[1], w2_scales[0])
+        load_scale_rows([nc.sync] * 4, ws_raw[0], w1_scales[0])
+        load_scale_rows([nc.sync] * 4, ws_raw[1], w2_scales[0])
+        nc.sync.dma_start(rdr_sb[:], rdr)
 
         w_dealt = [keep.tile([P, PACK, 2 * P], U8, name="w_dealt%d" % j, align_bytes=64) for j in range(2)]
         ws_dealt = [keep.tile([P, PACK, P], U8, name="ws_dealt%d" % j, align_bytes=64) for j in range(2)]
@@ -79,19 +80,18 @@ def tile_picked_ywvres_zero_p_kernel(tc, x_words, x_scales, w1_words, w1_scales,
             out=x_scale[:].rearrange("p h (d v) -> p h d v", d=D),
             in_=picked_scales[:].rearrange("p (h v d) -> p h d v", h=HALVES, d=D),
         )
-        deal_scales(0)
+        for h in range(HALVES):
+            nc.vector.tensor_copy(
+                out=x_code[h][:].rearrange("p (d v) -> p v d", d=D),
+                in_=table_words[:].bitcast(U32).indirect(offs_sb[:, h * (SH // 16) : (h + 1) * (SH // 16)]),
+            )
+            deal_scales(h)
         w3_sb = w_raw[0][:, 0 : 2 * N]
         w3s_sb = ws_raw[0][:, 0:N]
         unit_sb = keep.tile([P, PACK], F32, name="w_raw1", align_bytes=64)
         nc.sync.dma_start(out=unit_sb[:], in_=unit.rearrange("(p t) o -> p (t o)", t=PACK))
         nc.sync.dma_start(out=w3_sb.bitcast(I32), in_=w3_words[0].bitcast(I32))
         load_scale_rows([nc.sync] * 4, w3s_sb, w3_scales[0])
-        for h in range(HALVES):
-            nc.vector.tensor_copy(
-                out=x_code[h][:].rearrange("p (d v) -> p v d", d=D),
-                in_=table_words[:].bitcast(U32).indirect(offs_sb[:, h * (SH // 16) : (h + 1) * (SH // 16)]),
-            )
-        deal_scales(1)
 
         def product(dst, j, t, h, cols, start, stop):
             nc.tensor.matmul_mx(
@@ -117,7 +117,7 @@ def tile_picked_ywvres_zero_p_kernel(tc, x_words, x_scales, w1_words, w1_scales,
         z_tanh = [keep.tile([P, PACK, VH], F32, name="z_tanh%d" % h) for h in range(HALVES)]
         z_term = keep.tile([P, HALVES, PACK, VH], F32, name="z_term")
         window = [keep.tile([P, 4, V], F32, name="window%d" % t) for t in range(PACK)]
-        fetched = keep.tile([P, PACK, R], BF16, name="fetched", align_bytes=64)
+        fetched = [keep.tile([P, PACK, RH], BF16, name="fetched%d" % c, align_bytes=64) for c in range(HALVES)]
 
         def values(t, h):
             y = ybanks.tile([P, D * VH], F32, name="y")
@@ -146,30 +146,32 @@ def tile_picked_ywvres_zero_p_kernel(tc, x_words, x_scales, w1_words, w1_scales,
                 out=z_term[:, h, :, :], in0=z_sum[h][:], scalar=1.0 / D, in1=z_tanh[h][:], op0=ALU.mult, op1=ALU.mult
             )
 
-        def inverse_scale(t):
+        def inverse_root(t):
             nc.scalar.activation(out=window[t][:, 2, :], in_=group_max[t // 2][:, t % 2, :], func=ACT.Abs_reciprocal_sqrt, bias=0.2)
+
+        def inverse_scale(t):
             nc.scalar.activation(out=window[t][:, 3, :], in_=window[t][:, 2, :], func=ACT.Square)
 
         def level_sum(t):
             y_sum = y_sum_sb[:, t, :] if t < 2 else y_sum_ps[:, t - 2, :]
             nc.vector.scalar_tensor_tensor(
-                out=window[t][:, 1, :], in0=y_sum, scalar=unit_sb[:, t : t + 1], in1=window[t][:, 3, :], op0=ALU.mult, op1=ALU.mult
+                out=window[t][:, 1, :].rearrange("p (h v) -> p h v", h=HALVES),
+                in0=y_sum.rearrange("p (h v) -> p h v", h=HALVES),
+                scalar=unit_sb[:, t : t + 1],
+                in1=z_term[:, :, t, :],
+                op0=ALU.mult,
+                op1=ALU.mult,
             )
 
         def group_value(t):
-            nc.vector.tensor_tensor(
-                out=window[t][:, 0, :].rearrange("p (h v) -> p h v", h=HALVES),
-                in0=window[t][:, 1, :].rearrange("p (h v) -> p h v", h=HALVES),
-                in1=z_term[:, :, t, :],
-                op=ALU.mult,
-            )
+            nc.vector.tensor_tensor(out=window[t][:, 0, :], in0=window[t][:, 1, :], in1=window[t][:, 3, :], op=ALU.mult)
 
-        def fetch(t, lo, hi, on_vector):
-            src = window[t][:].rearrange("p a v -> p (a v)").indirect(rdr_sb[:, lo // 16 : hi // 16])
+        def fetch(t, c, on_vector):
+            src = window[t][:].rearrange("p a v -> p (a v)").indirect(rdr_sb[:, c * (RH // 16) : (c + 1) * (RH // 16)])
             if on_vector:
-                nc.vector.tensor_copy(out=fetched[:, t, lo:hi], in_=src)
+                nc.vector.tensor_copy(out=fetched[c][:, t, :], in_=src)
             else:
-                nc.scalar.activation(out=fetched[:, t, lo:hi], in_=src, func=ACT.Copy)
+                nc.scalar.activation(out=fetched[c][:, t, :], in_=src, func=ACT.Copy)
 
         for t in range(PACK):
             values(t, 0)
@@ -193,29 +195,39 @@ def tile_picked_ywvres_zero_p_kernel(tc, x_words, x_scales, w1_words, w1_scales,
             for h in range(HALVES):
                 group_sum(y_sum_ps[:, t - 2, h * VH : (h + 1) * VH], 0, t, h)
         for t in range(PACK):
-            inverse_scale(t)
-        level_sum(0)
-        level_sum(1)
-        group_value(0)
-        group_value(1)
-        level_sum(2)
-        level_sum(3)
-        group_value(2)
-        group_value(3)
-        fetch(0, 0, RH, False)
-        fetch(1, 0, RH, False)
-        fetch(2, 0, RH, True)
-        fetch(3, 0, RH, True)
+            level_sum(t)
+        inverse_root(0)
         for t in range(PACK):
-            fetch(t, RH, R, False)
+            if t + 1 < PACK:
+                inverse_root(t + 1)
+            inverse_scale(t)
 
         woven = [keep.tile([P, RH, PACK], BF16, name="woven%d" % c, align_bytes=64) for c in range(HALVES)]
         hid_code = [keep.tile([P, RH], U32, name="hid_code%d" % c, align_bytes=64) for c in range(HALVES)]
         hid_scale = [keep.tile([P, RH], U8, name="hid_scale%d" % c, align_bytes=64) for c in range(HALVES)]
-        for c in range(HALVES):
-            nc.vector.tensor_copy(out=woven[c][:], in_=fetched[:, :, c * RH : (c + 1) * RH].rearrange("p t r -> p r t"))
-        for c in range(HALVES):
+
+        def weave(c):
+            nc.vector.tensor_copy(out=woven[c][:], in_=fetched[c][:].rearrange("p t r -> p r t"))
+
+        def quantise(c):
             nc.vector.quantize_mx(out=hid_code[c][:].bitcast(FP8X4), scales=hid_scale[c][:], in_=woven[c][:].rearrange("p r t -> p (r t)"))
+
+        group_value(0)
+        group_value(1)
+        fetch(0, 0, True)
+        group_value(2)
+        group_value(3)
+        fetch(1, 0, False)
+        fetch(2, 0, False)
+        fetch(3, 0, True)
+        fetch(0, 1, False)
+        fetch(1, 1, False)
+        fetch(2, 1, False)
+        weave(0)
+        fetch(3, 1, True)
+        quantise(0)
+        weave(1)
+        quantise(1)
         for c in range(HALVES):
             acc = ybanks.tile([P, D * VH], F32, name="y")
             nc.tensor.matmul_mx(

@@ -21,6 +21,7 @@ HALVES = 2
 VH = V // HALVES
 SH = S // HALVES
 RH = R // HALVES
+CLEAR_SPLIT = 1536
 FLOPS = 2 * K * H * S * 2 + 2 * H * N * R
 
 
@@ -41,24 +42,27 @@ def tile_picked_ywvres_zero_p_kernel(tc, x_words, x_scales, w1_words, w1_scales,
         table_words = keep.tile([P, T], I32, name="table_words", align_bytes=64)
         table_scales = keep.tile([P, T], U8, name="table_scales", align_bytes=64)
         w_raw = [keep.tile([P, 2 * H], U8, name="w_raw%d" % j, align_bytes=64) for j in range(2)]
-        ws_raw = [keep.tile([P, H], U8, name="ws_raw%d" % j, align_bytes=64) for j in range(2)]
+        ws_raw = keep.tile([P, 2, H], U8, name="ws_raw", align_bytes=64)
+        w3_sb = keep.tile([P, 2 * N], U8, name="w3_sb", align_bytes=64)
+        unit_sb = keep.tile([P, PACK], F32, name="unit_sb")
 
-        nc.gpsimd.memset(table_scales[:, 0 : T // 2].bitcast(I32), 0)
-        nc.vector.memset(table_scales[:, T // 2 : T].bitcast(I32), 0)
-        for j in range(2):
-            nc.gpsimd.memset(ws_raw[j][:].bitcast(I32), 0)
+        nc.gpsimd.memset(ws_raw[:].rearrange("p j c -> p (j c)").bitcast(I32), 0)
+        nc.gpsimd.memset(table_scales[:, 0:CLEAR_SPLIT].bitcast(I32), 0)
+        nc.vector.memset(table_scales[:, CLEAR_SPLIT:T].bitcast(I32), 0)
 
         nc.sync.dma_start(offs_sb[:], offs)
         nc.sync.dma_start(out=w_raw[0][:].bitcast(I32), in_=w1_words[0].bitcast(I32))
         nc.sync.dma_start(out=w_raw[1][:].bitcast(I32), in_=w2_words[0].bitcast(I32))
-        load_scale_rows([nc.sync] * 4, table_scales, x_scales[0])
-        nc.sync.dma_start(out=table_words[:], in_=x_words[0].rearrange("p n t -> p (n t)").bitcast(I32))
-        load_scale_rows([nc.sync] * 4, ws_raw[0], w1_scales[0])
-        load_scale_rows([nc.sync] * 4, ws_raw[1], w2_scales[0])
         nc.sync.dma_start(rdr_sb[:], rdr)
+        nc.sync.dma_start(out=table_scales[0:P:8, :].bitcast(I32), in_=x_scales[0].bitcast(I32))
+        nc.sync.dma_start(out=ws_raw[0:P:8, 0, :].bitcast(I32), in_=w1_scales[0].bitcast(I32))
+        nc.sync.dma_start(out=ws_raw[0:P:8, 1, :].bitcast(I32), in_=w2_scales[0].bitcast(I32))
+        nc.sync.dma_start(out=table_words[:], in_=x_words[0].rearrange("p n t -> p (n t)").bitcast(I32))
+        nc.gpsimd.dma_start(out=unit_sb[:], in_=unit.rearrange("(p t) o -> p (t o)", t=PACK))
+        nc.gpsimd.dma_start(out=w3_sb[:].bitcast(I32), in_=w3_words[0].bitcast(I32))
 
         w_dealt = [keep.tile([P, PACK, 2 * P], U8, name="w_dealt%d" % j, align_bytes=64) for j in range(2)]
-        ws_dealt = [keep.tile([P, PACK, P], U8, name="ws_dealt%d" % j, align_bytes=64) for j in range(2)]
+        ws_dealt = keep.tile([P, 2 * H], U8, name="ws_dealt", align_bytes=64)
 
         def deal_words(j):
             nc.vector.tensor_copy(
@@ -66,40 +70,54 @@ def tile_picked_ywvres_zero_p_kernel(tc, x_words, x_scales, w1_words, w1_scales,
                 in_=w_raw[j][:].rearrange("p (m t b) -> p t m b", t=PACK, b=2),
             )
 
-        def deal_scales(j):
-            nc.vector.tensor_copy(out=ws_dealt[j][:], in_=ws_raw[j][:].rearrange("p (m t) -> p t m", t=PACK))
+        def close_up_rows(plane):
+            for r in range(1, 4):
+                nc.scalar.dma_start(out=plane[r:P:32, :].bitcast(I32), in_=plane[8 * r : P : 32, :].bitcast(I32))
 
-        picked_scales = keep.tile([P, S], U8, name="picked_scales", align_bytes=64)
-        x_scale = keep.tile([P, HALVES, D * VH], U8, name="x_scale", align_bytes=64)
+        picked_scales = [keep.tile([P, SH], U8, name="picked_scales%d" % h, align_bytes=64) for h in range(HALVES)]
+        x_scale = [keep.tile([P, SH], U8, name="x_scale%d" % h, align_bytes=64) for h in range(HALVES)]
         x_code = [keep.tile([P, D * VH], U32, name="x_code%d" % h, align_bytes=64) for h in range(HALVES)]
 
+        def pick_scales(h):
+            nc.vector.tensor_copy(out=picked_scales[h][:], in_=table_scales[:].indirect(offs_sb[:, h * (SH // 16) : (h + 1) * (SH // 16)]))
+
+        def deal_picked_scales(h):
+            nc.vector.tensor_copy(
+                out=x_scale[h][:].rearrange("p (d v) -> p d v", d=D),
+                in_=picked_scales[h][:].rearrange("p (v d) -> p d v", d=D),
+            )
+            close_up_rows(x_scale[h])
+
+        unit_mean = keep.tile([P, PACK], F32, name="unit_mean")
+        nc.scalar.activation(out=unit_mean[:], in_=unit_sb[:], func=ACT.Copy, scale=1.0 / D)
+
         deal_words(0)
-        deal_words(1)
-        nc.vector.tensor_copy(out=picked_scales[:], in_=table_scales[:].indirect(offs_sb[:]))
+        pick_scales(0)
+        deal_picked_scales(0)
         nc.vector.tensor_copy(
-            out=x_scale[:].rearrange("p h (d v) -> p h d v", d=D),
-            in_=picked_scales[:].rearrange("p (h v d) -> p h d v", h=HALVES, d=D),
+            out=ws_dealt[:].rearrange("p (j t m) -> p j t m", j=2, t=PACK),
+            in_=ws_raw[:].rearrange("p j (m t) -> p j t m", t=PACK),
         )
+        close_up_rows(ws_dealt)
+        pick_scales(1)
+        deal_picked_scales(1)
+        deal_words(1)
         for h in range(HALVES):
             nc.vector.tensor_copy(
                 out=x_code[h][:].rearrange("p (d v) -> p v d", d=D),
                 in_=table_words[:].bitcast(U32).indirect(offs_sb[:, h * (SH // 16) : (h + 1) * (SH // 16)]),
             )
-            deal_scales(h)
-        w3_sb = w_raw[0][:, 0 : 2 * N]
-        w3s_sb = ws_raw[0][:, 0:N]
-        unit_sb = keep.tile([P, PACK], F32, name="w_raw1", align_bytes=64)
-        nc.sync.dma_start(out=unit_sb[:], in_=unit.rearrange("(p t) o -> p (t o)", t=PACK))
-        nc.sync.dma_start(out=w3_sb.bitcast(I32), in_=w3_words[0].bitcast(I32))
+        w3s_sb = keep.tile([P, N], U8, name="table_words", align_bytes=64)
+        nc.gpsimd.memset(w3s_sb[:].bitcast(I32), 0)
         load_scale_rows([nc.sync] * 4, w3s_sb, w3_scales[0])
 
         def product(dst, j, t, h, cols, start, stop):
             nc.tensor.matmul_mx(
                 out=dst,
                 lhsT=w_dealt[j][:, t, :].bitcast(FP4X4),
-                lhsT_scale=ws_dealt[j][:, t, :],
+                lhsT_scale=ws_dealt[:, j * H + t * P : j * H + (t + 1) * P],
                 rhs=x_code[h][:, cols].bitcast(FP8X4),
-                rhs_scale=x_scale[:, h, cols],
+                rhs_scale=x_scale[h][:, cols],
                 start=start,
                 stop=stop,
             )
@@ -108,33 +126,35 @@ def tile_picked_ywvres_zero_p_kernel(tc, x_words, x_scales, w1_words, w1_scales,
             for d in range(D):
                 product(dst, j, t, h, slice(d * VH, (d + 1) * VH), d == 0, d == D - 1)
 
-        magnitude = [[keep.tile([P, 2, D * VH], F32, name="magnitude%d%d" % (h, tp)) for tp in range(2)] for h in range(HALVES)]
-        pair_max = [[keep.tile([P, 2, 2 * VH], F32, name="pair_max%d%d" % (h, tp)) for tp in range(2)] for h in range(HALVES)]
-        group_max = [keep.tile([P, 2, V], F32, name="group_max%d" % tp) for tp in range(2)]
+        magnitude = [keep.tile([P, PACK, D * VH], F32, name="magnitude%d" % h) for h in range(HALVES)]
+        pair_max = [keep.tile([P, PACK, 2 * VH], F32, name="pair_max%d" % h) for h in range(HALVES)]
+        group_max = keep.tile([P, PACK, V], F32, name="group_max")
+        root = keep.tile([P, PACK, V], F32, name="root")
+        inverse = keep.tile([P, PACK, V], F32, name="inverse")
         y_sum_sb = keep.tile([P, 2, V], F32, name="y_sum_sb")
         y_sum_ps = fixed.tile([P, 2, V], F32, name="y_sum_ps")
         z_sum = [fixed.tile([P, PACK, VH], F32, name="z_sum%d" % h) for h in range(HALVES)]
         z_tanh = [keep.tile([P, PACK, VH], F32, name="z_tanh%d" % h) for h in range(HALVES)]
         z_term = keep.tile([P, HALVES, PACK, VH], F32, name="z_term")
-        window = [keep.tile([P, 4, V], F32, name="window%d" % t) for t in range(PACK)]
+        window = [keep.tile([P, 2, V], F32, name="window%d" % t) for t in range(PACK)]
         fetched = [keep.tile([P, PACK, RH], BF16, name="fetched%d" % c, align_bytes=64) for c in range(HALVES)]
 
         def values(t, h):
             y = ybanks.tile([P, D * VH], F32, name="y")
             product(y[:], 0, t, h, slice(0, D * VH), True, True)
-            nc.scalar.activation(out=magnitude[h][t // 2][:, t % 2, :], in_=y[:], func=ACT.Abs)
+            nc.scalar.activation(out=magnitude[h][:, t, :], in_=y[:], func=ACT.Abs)
             if t < 2:
                 nc.vector.tensor_reduce(
                     out=y_sum_sb[:, t, h * VH : (h + 1) * VH], in_=y[:].rearrange("p (d v) -> p v d", d=D), axis=AX.X, op=ALU.add
                 )
 
-        def first_max(h, tp):
-            mag = magnitude[h][tp]
-            nc.vector.tensor_tensor(out=pair_max[h][tp][:], in0=mag[:, :, 0 : 2 * VH], in1=mag[:, :, 2 * VH : 4 * VH], op=ALU.max)
+        def first_max(h, lo, hi):
+            mag = magnitude[h]
+            nc.vector.tensor_tensor(out=pair_max[h][:, lo:hi, :], in0=mag[:, lo:hi, 0 : 2 * VH], in1=mag[:, lo:hi, 2 * VH : 4 * VH], op=ALU.max)
 
-        def second_max(h, tp):
-            pm = pair_max[h][tp]
-            nc.vector.tensor_tensor(out=group_max[tp][:, :, h * VH : (h + 1) * VH], in0=pm[:, :, 0:VH], in1=pm[:, :, VH : 2 * VH], op=ALU.max)
+        def second_max(h):
+            pm = pair_max[h]
+            nc.vector.tensor_tensor(out=group_max[:, :, h * VH : (h + 1) * VH], in0=pm[:, :, 0:VH], in1=pm[:, :, VH : 2 * VH], op=ALU.max)
 
         def zero_points(h):
             for t in range(PACK):
@@ -142,29 +162,29 @@ def tile_picked_ywvres_zero_p_kernel(tc, x_words, x_scales, w1_words, w1_scales,
             nc.scalar.activation(out=z_tanh[h][:], in_=z_sum[h][:], func=ACT.Tanh, scale=1.0 / D)
 
         def zero_term(h):
-            nc.vector.scalar_tensor_tensor(
-                out=z_term[:, h, :, :], in0=z_sum[h][:], scalar=1.0 / D, in1=z_tanh[h][:], op0=ALU.mult, op1=ALU.mult
-            )
+            nc.vector.tensor_tensor(out=z_term[:, h, :, :], in0=z_sum[h][:], in1=z_tanh[h][:], op=ALU.mult)
 
-        def inverse_root(t):
-            nc.scalar.activation(out=window[t][:, 2, :], in_=group_max[t // 2][:, t % 2, :], func=ACT.Abs_reciprocal_sqrt, bias=0.2)
+        def inverse_root(tp):
+            pair = slice(2 * tp, 2 * tp + 2)
+            nc.scalar.activation(out=root[:, pair, :], in_=group_max[:, pair, :], func=ACT.Abs_reciprocal_sqrt, bias=0.2)
 
-        def inverse_scale(t):
-            nc.scalar.activation(out=window[t][:, 3, :], in_=window[t][:, 2, :], func=ACT.Square)
+        def inverse_scale(tp):
+            pair = slice(2 * tp, 2 * tp + 2)
+            nc.scalar.activation(out=inverse[:, pair, :], in_=root[:, pair, :], func=ACT.Square)
 
         def level_sum(t):
             y_sum = y_sum_sb[:, t, :] if t < 2 else y_sum_ps[:, t - 2, :]
             nc.vector.scalar_tensor_tensor(
                 out=window[t][:, 1, :].rearrange("p (h v) -> p h v", h=HALVES),
                 in0=y_sum.rearrange("p (h v) -> p h v", h=HALVES),
-                scalar=unit_sb[:, t : t + 1],
+                scalar=unit_mean[:, t : t + 1],
                 in1=z_term[:, :, t, :],
                 op0=ALU.mult,
                 op1=ALU.mult,
             )
 
         def group_value(t):
-            nc.vector.tensor_tensor(out=window[t][:, 0, :], in0=window[t][:, 1, :], in1=window[t][:, 3, :], op=ALU.mult)
+            nc.vector.tensor_tensor(out=window[t][:, 0, :], in0=window[t][:, 1, :], in1=inverse[:, t, :], op=ALU.mult)
 
         def fetch(t, c, on_vector):
             src = window[t][:].rearrange("p a v -> p (a v)").indirect(rdr_sb[:, c * (RH // 16) : (c + 1) * (RH // 16)])
@@ -178,18 +198,15 @@ def tile_picked_ywvres_zero_p_kernel(tc, x_words, x_scales, w1_words, w1_scales,
         values(0, 1)
         values(1, 1)
         zero_points(0)
-        first_max(0, 0)
-        first_max(0, 1)
+        first_max(0, 0, 2)
+        first_max(0, 2, 4)
         values(2, 1)
         values(3, 1)
         zero_points(1)
-        second_max(0, 0)
-        first_max(1, 0)
-        second_max(0, 1)
-        second_max(1, 0)
-        first_max(1, 1)
+        second_max(0)
+        first_max(1, 0, 4)
         zero_term(0)
-        second_max(1, 1)
+        second_max(1)
         zero_term(1)
         for t in (2, 3):
             for h in range(HALVES):
@@ -197,10 +214,9 @@ def tile_picked_ywvres_zero_p_kernel(tc, x_words, x_scales, w1_words, w1_scales,
         for t in range(PACK):
             level_sum(t)
         inverse_root(0)
-        for t in range(PACK):
-            if t + 1 < PACK:
-                inverse_root(t + 1)
-            inverse_scale(t)
+        inverse_root(1)
+        inverse_scale(0)
+        inverse_scale(1)
 
         woven = [keep.tile([P, RH, PACK], BF16, name="woven%d" % c, align_bytes=64) for c in range(HALVES)]
         hid_code = [keep.tile([P, RH], U32, name="hid_code%d" % c, align_bytes=64) for c in range(HALVES)]
@@ -212,28 +228,20 @@ def tile_picked_ywvres_zero_p_kernel(tc, x_words, x_scales, w1_words, w1_scales,
         def quantise(c):
             nc.vector.quantize_mx(out=hid_code[c][:].bitcast(FP8X4), scales=hid_scale[c][:], in_=woven[c][:].rearrange("p r t -> p (r t)"))
 
-        group_value(0)
-        group_value(1)
-        fetch(0, 0, True)
-        group_value(2)
-        group_value(3)
-        fetch(1, 0, False)
-        fetch(2, 0, False)
-        fetch(3, 0, True)
-        fetch(0, 1, False)
-        fetch(1, 1, False)
-        fetch(2, 1, False)
-        weave(0)
-        fetch(3, 1, True)
-        quantise(0)
-        weave(1)
-        quantise(1)
+        for t in range(PACK):
+            group_value(t)
+        for c in range(HALVES):
+            for t in range(PACK):
+                fetch(t, c, t == PACK - 1)
+        for c in range(HALVES):
+            weave(c)
+            quantise(c)
         for c in range(HALVES):
             acc = ybanks.tile([P, D * VH], F32, name="y")
             nc.tensor.matmul_mx(
                 out=acc[:, 0:RH],
-                lhsT=w3_sb.bitcast(FP4X4),
-                lhsT_scale=w3s_sb,
+                lhsT=w3_sb[:].bitcast(FP4X4),
+                lhsT_scale=w3s_sb[:],
                 rhs=hid_code[c][:].bitcast(FP8X4),
                 rhs_scale=hid_scale[c][:],
                 start=True,

@@ -15,30 +15,42 @@ ALU = mybir.AluOpType
 AX = mybir.AxisListType
 
 P = 128
-K, T, S, D, N, H, V, R = 512, 4096, 1024, 4, 128, 512, 256, 512
+K = 512
+T = 4096
+S = 1024
+D = 4
+V = S // D
+H = 512
+N = 128
+R = 512
 PACK = 4
+LIST_ROWS = 16
+QUADRANT = 32
+BLOCK_PARTS = 8
 HALVES = 2
-VH = V // HALVES
 SH = S // HALVES
-RH = R // HALVES
+VH = V // HALVES
+SCALE_FLOOR = 0.2
+
+SUMMED_ON_VECTOR = 2
 CLEAR_SPLIT = 1536
+PIECES = ((0, 256), (256, 384), (384, 512))
+TURN_BANKS = 5
+
 FLOPS = 2 * K * H * S * 2 + 2 * H * N * R
 
 
-def load_scale_rows(queues, plane, rows):
-    for q in range(4):
-        queues[q].dma_start(out=plane[32 * q : 32 * q + 4, :].bitcast(I32), in_=rows[4 * q : 4 * q + 4, :].bitcast(I32))
-
-
-def tile_picked_ywvres_zero_p_kernel(tc, x_words, x_scales, w1_words, w1_scales, w2_words, w2_scales, unit, w3_words, w3_scales, offs, rdr, out):
+def tile_picked_ywvres_zero_p_kernel(
+    tc, x_words, x_scales, w1_words, w1_scales, w2_words, w2_scales, unit, w3_words, w3_scales, offs, rdr, out
+):
     nc = tc.nc
     with ExitStack() as ctx:
         keep = ctx.enter_context(tc.tile_pool(name="keep", bufs=1))
-        ybanks = ctx.enter_context(tc.psum_pool(name="ybanks", bufs=5))
-        fixed = ctx.enter_context(tc.psum_pool(name="fixed", bufs=1))
+        turn_banks = ctx.enter_context(tc.psum_pool(name="turn_banks", bufs=TURN_BANKS))
+        sum_banks = ctx.enter_context(tc.psum_pool(name="sum_banks", bufs=1))
 
-        offs_sb = keep.tile([P, S // 16], U16, name="offs_sb")
-        rdr_sb = keep.tile([P, R // 16], U16, name="rdr_sb")
+        offs_sb = keep.tile([P, S // LIST_ROWS], U16, name="offs_sb")
+        rdr_sb = keep.tile([P, R // LIST_ROWS], U16, name="rdr_sb")
         table_words = keep.tile([P, T], I32, name="table_words", align_bytes=64)
         table_scales = keep.tile([P, T], U8, name="table_scales", align_bytes=64)
         w_raw = [keep.tile([P, 2 * H], U8, name="w_raw%d" % j, align_bytes=64) for j in range(2)]
@@ -51,65 +63,62 @@ def tile_picked_ywvres_zero_p_kernel(tc, x_words, x_scales, w1_words, w1_scales,
         nc.vector.memset(table_scales[:, CLEAR_SPLIT:T].bitcast(I32), 0)
 
         nc.sync.dma_start(offs_sb[:], offs)
+        nc.sync.dma_start(out=unit_sb[:], in_=unit.rearrange("(p t) o -> p (t o)", t=PACK))
         nc.sync.dma_start(out=w_raw[0][:].bitcast(I32), in_=w1_words[0].bitcast(I32))
         nc.sync.dma_start(out=w_raw[1][:].bitcast(I32), in_=w2_words[0].bitcast(I32))
-        nc.sync.dma_start(rdr_sb[:], rdr)
-        nc.sync.dma_start(out=table_scales[0:P:8, :].bitcast(I32), in_=x_scales[0].bitcast(I32))
-        nc.sync.dma_start(out=ws_raw[0:P:8, 0, :].bitcast(I32), in_=w1_scales[0].bitcast(I32))
-        nc.sync.dma_start(out=ws_raw[0:P:8, 1, :].bitcast(I32), in_=w2_scales[0].bitcast(I32))
+        nc.sync.dma_start(out=ws_raw[0:P:BLOCK_PARTS, 0, :].bitcast(I32), in_=w1_scales[0].bitcast(I32))
+        nc.sync.dma_start(out=ws_raw[0:P:BLOCK_PARTS, 1, :].bitcast(I32), in_=w2_scales[0].bitcast(I32))
+        nc.sync.dma_start(out=table_scales[0:P:BLOCK_PARTS, :].bitcast(I32), in_=x_scales[0].bitcast(I32))
         nc.sync.dma_start(out=table_words[:], in_=x_words[0].rearrange("p n t -> p (n t)").bitcast(I32))
-        nc.gpsimd.dma_start(out=unit_sb[:], in_=unit.rearrange("(p t) o -> p (t o)", t=PACK))
+        nc.sync.dma_start(rdr_sb[:], rdr)
         nc.gpsimd.dma_start(out=w3_sb[:].bitcast(I32), in_=w3_words[0].bitcast(I32))
 
         w_dealt = [keep.tile([P, PACK, 2 * P], U8, name="w_dealt%d" % j, align_bytes=64) for j in range(2)]
         ws_dealt = keep.tile([P, 2 * H], U8, name="ws_dealt", align_bytes=64)
+        picked_scales = keep.tile([P, S], U8, name="picked_scales", align_bytes=64)
+        x_scale = keep.tile([P, S], U8, name="x_scale", align_bytes=64)
+        x_code = [keep.tile([P, SH], U32, name="x_code%d" % h, align_bytes=64) for h in range(HALVES)]
 
-        def deal_words(j):
-            nc.vector.tensor_copy(
-                out=w_dealt[j][:].rearrange("p t (m b) -> p t m b", b=2),
-                in_=w_raw[j][:].rearrange("p (m t b) -> p t m b", t=PACK, b=2),
-            )
-
-        def close_up_rows(plane):
-            for r in range(1, 4):
-                nc.scalar.dma_start(out=plane[r:P:32, :].bitcast(I32), in_=plane[8 * r : P : 32, :].bitcast(I32))
-
-        picked_scales = [keep.tile([P, SH], U8, name="picked_scales%d" % h, align_bytes=64) for h in range(HALVES)]
-        x_scale = [keep.tile([P, SH], U8, name="x_scale%d" % h, align_bytes=64) for h in range(HALVES)]
-        x_code = [keep.tile([P, D * VH], U32, name="x_code%d" % h, align_bytes=64) for h in range(HALVES)]
-
-        def pick_scales(h):
-            nc.vector.tensor_copy(out=picked_scales[h][:], in_=table_scales[:].indirect(offs_sb[:, h * (SH // 16) : (h + 1) * (SH // 16)]))
-
-        def deal_picked_scales(h):
-            nc.vector.tensor_copy(
-                out=x_scale[h][:].rearrange("p (d v) -> p d v", d=D),
-                in_=picked_scales[h][:].rearrange("p (v d) -> p d v", d=D),
-            )
-            close_up_rows(x_scale[h])
+        def close_up_rows(scales):
+            for r in range(1, QUADRANT // BLOCK_PARTS):
+                nc.scalar.dma_start(
+                    out=scales[r:P:QUADRANT, :].bitcast(I32), in_=scales[BLOCK_PARTS * r : P : QUADRANT, :].bitcast(I32)
+                )
 
         unit_mean = keep.tile([P, PACK], F32, name="unit_mean")
         nc.scalar.activation(out=unit_mean[:], in_=unit_sb[:], func=ACT.Copy, scale=1.0 / D)
 
-        deal_words(0)
-        pick_scales(0)
-        deal_picked_scales(0)
         nc.vector.tensor_copy(
             out=ws_dealt[:].rearrange("p (j t m) -> p j t m", j=2, t=PACK),
             in_=ws_raw[:].rearrange("p j (m t) -> p j t m", t=PACK),
         )
         close_up_rows(ws_dealt)
-        pick_scales(1)
-        deal_picked_scales(1)
-        deal_words(1)
+
+        nc.vector.tensor_copy(out=picked_scales[:], in_=table_scales[:].indirect(offs_sb[:]))
+        nc.vector.tensor_copy(
+            out=x_scale[:].rearrange("p (h d v) -> p h d v", h=HALVES, d=D),
+            in_=picked_scales[:].rearrange("p (h v d) -> p h d v", h=HALVES, d=D),
+        )
+        close_up_rows(x_scale)
+
+        for j in range(2):
+            nc.vector.tensor_copy(
+                out=w_dealt[j][:].rearrange("p t (m b) -> p t m b", b=2),
+                in_=w_raw[j][:].rearrange("p (m t b) -> p t m b", t=PACK, b=2),
+            )
+
         for h in range(HALVES):
             nc.vector.tensor_copy(
                 out=x_code[h][:].rearrange("p (d v) -> p v d", d=D),
-                in_=table_words[:].bitcast(U32).indirect(offs_sb[:, h * (SH // 16) : (h + 1) * (SH // 16)]),
+                in_=table_words[:].bitcast(U32).indirect(offs_sb[:, h * (SH // LIST_ROWS) : (h + 1) * (SH // LIST_ROWS)]),
             )
+
         w3s_sb = keep.tile([P, N], U8, name="table_words", align_bytes=64)
         nc.gpsimd.memset(w3s_sb[:].bitcast(I32), 0)
-        load_scale_rows([nc.sync] * 4, w3s_sb, w3_scales[0])
+        for q in range(P // QUADRANT):
+            nc.sync.dma_start(
+                out=w3s_sb[QUADRANT * q : QUADRANT * q + 4, :].bitcast(I32), in_=w3_scales[0][4 * q : 4 * q + 4, :].bitcast(I32)
+            )
 
         def product(dst, j, t, h, cols, start, stop):
             nc.tensor.matmul_mx(
@@ -117,7 +126,7 @@ def tile_picked_ywvres_zero_p_kernel(tc, x_words, x_scales, w1_words, w1_scales,
                 lhsT=w_dealt[j][:, t, :].bitcast(FP4X4),
                 lhsT_scale=ws_dealt[:, j * H + t * P : j * H + (t + 1) * P],
                 rhs=x_code[h][:, cols].bitcast(FP8X4),
-                rhs_scale=x_scale[h][:, cols],
+                rhs_scale=x_scale[:, h * SH + cols.start : h * SH + cols.stop],
                 start=start,
                 stop=stop,
             )
@@ -126,35 +135,37 @@ def tile_picked_ywvres_zero_p_kernel(tc, x_words, x_scales, w1_words, w1_scales,
             for d in range(D):
                 product(dst, j, t, h, slice(d * VH, (d + 1) * VH), d == 0, d == D - 1)
 
-        magnitude = [keep.tile([P, PACK, D * VH], F32, name="magnitude%d" % h) for h in range(HALVES)]
+        magnitude = [keep.tile([P, PACK, SH], F32, name="magnitude%d" % h) for h in range(HALVES)]
         pair_max = [keep.tile([P, PACK, 2 * VH], F32, name="pair_max%d" % h) for h in range(HALVES)]
         group_max = keep.tile([P, PACK, V], F32, name="group_max")
         root = keep.tile([P, PACK, V], F32, name="root")
         inverse = keep.tile([P, PACK, V], F32, name="inverse")
-        y_sum_sb = keep.tile([P, 2, V], F32, name="y_sum_sb")
-        y_sum_ps = fixed.tile([P, 2, V], F32, name="y_sum_ps")
-        z_sum = [fixed.tile([P, PACK, VH], F32, name="z_sum%d" % h) for h in range(HALVES)]
+        y_sum_sb = keep.tile([P, SUMMED_ON_VECTOR, V], F32, name="y_sum_sb")
+        y_sum_ps = sum_banks.tile([P, PACK - SUMMED_ON_VECTOR, V], F32, name="y_sum_ps")
+        z_sum = [sum_banks.tile([P, PACK, VH], F32, name="z_sum%d" % h) for h in range(HALVES)]
         z_tanh = [keep.tile([P, PACK, VH], F32, name="z_tanh%d" % h) for h in range(HALVES)]
         z_term = keep.tile([P, HALVES, PACK, VH], F32, name="z_term")
         window = [keep.tile([P, 2, V], F32, name="window%d" % t) for t in range(PACK)]
-        fetched = [keep.tile([P, PACK, RH], BF16, name="fetched%d" % c, align_bytes=64) for c in range(HALVES)]
+        fetched = [keep.tile([P, PACK, hi - lo], BF16, name="fetched%d" % c, align_bytes=64) for c, (lo, hi) in enumerate(PIECES)]
 
         def values(t, h):
-            y = ybanks.tile([P, D * VH], F32, name="y")
-            product(y[:], 0, t, h, slice(0, D * VH), True, True)
+            y = turn_banks.tile([P, SH], F32, name="turn")
+            product(y[:], 0, t, h, slice(0, SH), True, True)
             nc.scalar.activation(out=magnitude[h][:, t, :], in_=y[:], func=ACT.Abs)
-            if t < 2:
+            if t < SUMMED_ON_VECTOR:
                 nc.vector.tensor_reduce(
                     out=y_sum_sb[:, t, h * VH : (h + 1) * VH], in_=y[:].rearrange("p (d v) -> p v d", d=D), axis=AX.X, op=ALU.add
                 )
 
-        def first_max(h, lo, hi):
-            mag = magnitude[h]
-            nc.vector.tensor_tensor(out=pair_max[h][:, lo:hi, :], in0=mag[:, lo:hi, 0 : 2 * VH], in1=mag[:, lo:hi, 2 * VH : 4 * VH], op=ALU.max)
+        def first_max(h, planes):
+            nc.vector.tensor_tensor(
+                out=pair_max[h][:, planes, :], in0=magnitude[h][:, planes, 0 : 2 * VH], in1=magnitude[h][:, planes, 2 * VH : SH], op=ALU.max
+            )
 
         def second_max(h):
-            pm = pair_max[h]
-            nc.vector.tensor_tensor(out=group_max[:, :, h * VH : (h + 1) * VH], in0=pm[:, :, 0:VH], in1=pm[:, :, VH : 2 * VH], op=ALU.max)
+            nc.vector.tensor_tensor(
+                out=group_max[:, :, h * VH : (h + 1) * VH], in0=pair_max[h][:, :, 0:VH], in1=pair_max[h][:, :, VH : 2 * VH], op=ALU.max
+            )
 
         def zero_points(h):
             for t in range(PACK):
@@ -164,16 +175,8 @@ def tile_picked_ywvres_zero_p_kernel(tc, x_words, x_scales, w1_words, w1_scales,
         def zero_term(h):
             nc.vector.tensor_tensor(out=z_term[:, h, :, :], in0=z_sum[h][:], in1=z_tanh[h][:], op=ALU.mult)
 
-        def inverse_root(tp):
-            pair = slice(2 * tp, 2 * tp + 2)
-            nc.scalar.activation(out=root[:, pair, :], in_=group_max[:, pair, :], func=ACT.Abs_reciprocal_sqrt, bias=0.2)
-
-        def inverse_scale(tp):
-            pair = slice(2 * tp, 2 * tp + 2)
-            nc.scalar.activation(out=inverse[:, pair, :], in_=root[:, pair, :], func=ACT.Square)
-
-        def level_sum(t):
-            y_sum = y_sum_sb[:, t, :] if t < 2 else y_sum_ps[:, t - 2, :]
+        def numerator(t):
+            y_sum = y_sum_sb[:, t, :] if t < SUMMED_ON_VECTOR else y_sum_ps[:, t - SUMMED_ON_VECTOR, :]
             nc.vector.scalar_tensor_tensor(
                 out=window[t][:, 1, :].rearrange("p (h v) -> p h v", h=HALVES),
                 in0=y_sum.rearrange("p (h v) -> p h v", h=HALVES),
@@ -183,63 +186,57 @@ def tile_picked_ywvres_zero_p_kernel(tc, x_words, x_scales, w1_words, w1_scales,
                 op1=ALU.mult,
             )
 
-        def group_value(t):
-            nc.vector.tensor_tensor(out=window[t][:, 0, :], in0=window[t][:, 1, :], in1=inverse[:, t, :], op=ALU.mult)
-
-        def fetch(t, c, on_vector):
-            src = window[t][:].rearrange("p a v -> p (a v)").indirect(rdr_sb[:, c * (RH // 16) : (c + 1) * (RH // 16)])
-            if on_vector:
-                nc.vector.tensor_copy(out=fetched[c][:, t, :], in_=src)
-            else:
-                nc.scalar.activation(out=fetched[c][:, t, :], in_=src, func=ACT.Copy)
-
+        low_planes, high_planes, all_planes = slice(0, 2), slice(2, PACK), slice(0, PACK)
         for t in range(PACK):
             values(t, 0)
         values(0, 1)
         values(1, 1)
         zero_points(0)
-        first_max(0, 0, 2)
-        first_max(0, 2, 4)
+        first_max(0, low_planes)
+        first_max(0, high_planes)
         values(2, 1)
         values(3, 1)
         zero_points(1)
         second_max(0)
-        first_max(1, 0, 4)
+        first_max(1, all_planes)
         zero_term(0)
         second_max(1)
         zero_term(1)
-        for t in (2, 3):
+        for t in range(SUMMED_ON_VECTOR, PACK):
             for h in range(HALVES):
-                group_sum(y_sum_ps[:, t - 2, h * VH : (h + 1) * VH], 0, t, h)
+                group_sum(y_sum_ps[:, t - SUMMED_ON_VECTOR, h * VH : (h + 1) * VH], 0, t, h)
         for t in range(PACK):
-            level_sum(t)
-        inverse_root(0)
-        inverse_root(1)
-        inverse_scale(0)
-        inverse_scale(1)
+            numerator(t)
 
-        woven = [keep.tile([P, RH, PACK], BF16, name="woven%d" % c, align_bytes=64) for c in range(HALVES)]
-        hid_code = [keep.tile([P, RH], U32, name="hid_code%d" % c, align_bytes=64) for c in range(HALVES)]
-        hid_scale = [keep.tile([P, RH], U8, name="hid_scale%d" % c, align_bytes=64) for c in range(HALVES)]
+        for planes in (low_planes, high_planes):
+            nc.scalar.activation(out=root[:, planes, :], in_=group_max[:, planes, :], func=ACT.Abs_reciprocal_sqrt, bias=SCALE_FLOOR)
+        for planes in (low_planes, high_planes):
+            nc.scalar.activation(out=inverse[:, planes, :], in_=root[:, planes, :], func=ACT.Square)
 
-        def weave(c):
+        woven = [keep.tile([P, hi - lo, PACK], BF16, name="woven%d" % c, align_bytes=64) for c, (lo, hi) in enumerate(PIECES)]
+        hid_code = [keep.tile([P, hi - lo], U32, name="hid_code%d" % c, align_bytes=64) for c, (lo, hi) in enumerate(PIECES)]
+        hid_scale = [keep.tile([P, hi - lo], U8, name="hid_scale%d" % c, align_bytes=64) for c, (lo, hi) in enumerate(PIECES)]
+
+        for t in range(PACK):
+            nc.vector.tensor_tensor(out=window[t][:, 0, :], in0=window[t][:, 1, :], in1=inverse[:, t, :], op=ALU.mult)
+
+        for c, (lo, hi) in enumerate(PIECES):
+            first_on_vector = PACK - 1 if c == 0 else PACK - 2
+            for t in range(PACK):
+                looked_up = window[t][:].rearrange("p a v -> p (a v)").indirect(rdr_sb[:, lo // LIST_ROWS : hi // LIST_ROWS])
+                if t >= first_on_vector:
+                    nc.vector.tensor_copy(out=fetched[c][:, t, :], in_=looked_up)
+                else:
+                    nc.scalar.activation(out=fetched[c][:, t, :], in_=looked_up, func=ACT.Copy)
+
+        for c in range(len(PIECES)):
             nc.vector.tensor_copy(out=woven[c][:], in_=fetched[c][:].rearrange("p t r -> p r t"))
-
-        def quantise(c):
             nc.vector.quantize_mx(out=hid_code[c][:].bitcast(FP8X4), scales=hid_scale[c][:], in_=woven[c][:].rearrange("p r t -> p (r t)"))
 
-        for t in range(PACK):
-            group_value(t)
-        for c in range(HALVES):
-            for t in range(PACK):
-                fetch(t, c, t == PACK - 1)
-        for c in range(HALVES):
-            weave(c)
-            quantise(c)
-        for c in range(HALVES):
-            acc = ybanks.tile([P, D * VH], F32, name="y")
+        for c, (lo, hi) in enumerate(PIECES):
+            acc = turn_banks.tile([P, SH], F32, name="turn")
             nc.tensor.matmul_mx(
-                out=acc[:, 0:RH],
+                out=acc[:, 0 : hi - lo],
                 lhsT=w3_sb[:].bitcast(FP4X4),
                 lhsT_scale=w3s_sb[:],
                 rhs=hid_code[c][:].bitcast(FP8X4),
@@ -247,6 +244,6 @@ def tile_picked_ywvres_zero_p_kernel(tc, x_words, x_scales, w1_words, w1_scales,
                 start=True,
                 stop=True,
             )
-            result = keep.tile([P, RH], F32, name="result%d" % c)
-            nc.scalar.copy(out=result[:], in_=acc[:, 0:RH])
-            nc.sync.dma_start(out=out[:, c * RH : (c + 1) * RH], in_=result[:])
+            result = keep.tile([P, hi - lo], F32, name="result%d" % c)
+            nc.scalar.copy(out=result[:], in_=acc[:, 0 : hi - lo])
+            nc.sync.dma_start(out=out[:, lo:hi], in_=result[:])

from contextlib import ExitStack

import concourse.mybir as mybir

F32 = mybir.dt.float32
BF16 = mybir.dt.bfloat16
I32 = mybir.dt.int32
U32 = mybir.dt.uint32
U16 = mybir.dt.uint16
U8 = mybir.dt.uint8
FP8X4 = mybir.dt.float8_e4m3fn_x4
FP4X4 = mybir.dt.float4_e2m1fn_x4
ACT = mybir.ActivationFunctionType
ALU = mybir.AluOpType
AX = mybir.AxisListType

P = 128
K = 512
T = 4096
S = 1024
D = 4
V = S // D
H = 512
N = 128
R = 512
PACK = 4
LIST_ROWS = 16
QUADRANT = 32
BLOCK_PARTS = 8
HALVES = 2
SH = S // HALVES
VH = V // HALVES
SCALE_FLOOR = 0.2

SUMMED_ON_VECTOR = 2
CLEAR_SPLIT = 1536
PIECES = ((0, 256), (256, 384), (384, 512))
TURN_BANKS = 5

FLOPS = 2 * K * H * S * 2 + 2 * H * N * R


def tile_picked_ywvres_zero_p_kernel(
    tc, x_words, x_scales, w1_words, w1_scales, w2_words, w2_scales, unit, w3_words, w3_scales, offs, rdr, out
):
    nc = tc.nc
    with ExitStack() as ctx:
        keep = ctx.enter_context(tc.tile_pool(name="keep", bufs=1))
        turn_banks = ctx.enter_context(tc.psum_pool(name="turn_banks", bufs=TURN_BANKS))
        sum_banks = ctx.enter_context(tc.psum_pool(name="sum_banks", bufs=1))

        offs_sb = keep.tile([P, S // LIST_ROWS], U16, name="offs_sb")
        rdr_sb = keep.tile([P, R // LIST_ROWS], U16, name="rdr_sb")
        table_words = keep.tile([P, T], I32, name="table_words", align_bytes=64)
        table_scales = keep.tile([P, T], U8, name="table_scales", align_bytes=64)
        w_raw = [keep.tile([P, 2 * H], U8, name="w_raw%d" % j, align_bytes=64) for j in range(2)]
        ws_raw = keep.tile([P, 2, H], U8, name="ws_raw", align_bytes=64)
        w3_sb = keep.tile([P, 2 * N], U8, name="w3_sb", align_bytes=64)
        unit_sb = keep.tile([P, PACK], F32, name="unit_sb")

        nc.gpsimd.memset(ws_raw[:].rearrange("p j c -> p (j c)").bitcast(I32), 0)
        nc.gpsimd.memset(table_scales[:, 0:CLEAR_SPLIT].bitcast(I32), 0)
        nc.vector.memset(table_scales[:, CLEAR_SPLIT:T].bitcast(I32), 0)

        nc.sync.dma_start(offs_sb[:], offs)
        nc.sync.dma_start(out=unit_sb[:], in_=unit.rearrange("(p t) o -> p (t o)", t=PACK))
        nc.sync.dma_start(out=w_raw[0][:].bitcast(I32), in_=w1_words[0].bitcast(I32))
        nc.sync.dma_start(out=w_raw[1][:].bitcast(I32), in_=w2_words[0].bitcast(I32))
        nc.sync.dma_start(out=ws_raw[0:P:BLOCK_PARTS, 0, :].bitcast(I32), in_=w1_scales[0].bitcast(I32))
        nc.sync.dma_start(out=ws_raw[0:P:BLOCK_PARTS, 1, :].bitcast(I32), in_=w2_scales[0].bitcast(I32))
        nc.sync.dma_start(out=table_scales[0:P:BLOCK_PARTS, :].bitcast(I32), in_=x_scales[0].bitcast(I32))
        nc.sync.dma_start(out=table_words[:], in_=x_words[0].rearrange("p n t -> p (n t)").bitcast(I32))
        nc.sync.dma_start(rdr_sb[:], rdr)
        nc.gpsimd.dma_start(out=w3_sb[:].bitcast(I32), in_=w3_words[0].bitcast(I32))

        w_dealt = [keep.tile([P, PACK, 2 * P], U8, name="w_dealt%d" % j, align_bytes=64) for j in range(2)]
        ws_dealt = keep.tile([P, 2 * H], U8, name="ws_dealt", align_bytes=64)
        picked_scales = keep.tile([P, S], U8, name="picked_scales", align_bytes=64)
        x_scale = keep.tile([P, S], U8, name="x_scale", align_bytes=64)
        x_code = [keep.tile([P, SH], U32, name="x_code%d" % h, align_bytes=64) for h in range(HALVES)]

        def close_up_rows(scales):
            for r in range(1, QUADRANT // BLOCK_PARTS):
                nc.scalar.dma_start(
                    out=scales[r:P:QUADRANT, :].bitcast(I32), in_=scales[BLOCK_PARTS * r : P : QUADRANT, :].bitcast(I32)
                )

        unit_mean = keep.tile([P, PACK], F32, name="unit_mean")
        nc.scalar.activation(out=unit_mean[:], in_=unit_sb[:], func=ACT.Copy, scale=1.0 / D)

        nc.vector.tensor_copy(
            out=ws_dealt[:].rearrange("p (j t m) -> p j t m", j=2, t=PACK),
            in_=ws_raw[:].rearrange("p j (m t) -> p j t m", t=PACK),
        )
        close_up_rows(ws_dealt)

        nc.vector.tensor_copy(out=picked_scales[:], in_=table_scales[:].indirect(offs_sb[:]))
        nc.vector.tensor_copy(
            out=x_scale[:].rearrange("p (h d v) -> p h d v", h=HALVES, d=D),
            in_=picked_scales[:].rearrange("p (h v d) -> p h d v", h=HALVES, d=D),
        )
        close_up_rows(x_scale)

        for j in range(2):
            nc.vector.tensor_copy(
                out=w_dealt[j][:].rearrange("p t (m b) -> p t m b", b=2),
                in_=w_raw[j][:].rearrange("p (m t b) -> p t m b", t=PACK, b=2),
            )

        for h in range(HALVES):
            nc.vector.tensor_copy(
                out=x_code[h][:].rearrange("p (d v) -> p v d", d=D),
                in_=table_words[:].bitcast(U32).indirect(offs_sb[:, h * (SH // LIST_ROWS) : (h + 1) * (SH // LIST_ROWS)]),
            )

        w3s_sb = keep.tile([P, N], U8, name="table_words", align_bytes=64)
        nc.gpsimd.memset(w3s_sb[:].bitcast(I32), 0)
        for q in range(P // QUADRANT):
            nc.sync.dma_start(
                out=w3s_sb[QUADRANT * q : QUADRANT * q + 4, :].bitcast(I32), in_=w3_scales[0][4 * q : 4 * q + 4, :].bitcast(I32)
            )

        def product(dst, j, t, h, cols, start, stop):
            nc.tensor.matmul_mx(
                out=dst,
                lhsT=w_dealt[j][:, t, :].bitcast(FP4X4),
                lhsT_scale=ws_dealt[:, j * H + t * P : j * H + (t + 1) * P],
                rhs=x_code[h][:, cols].bitcast(FP8X4),
                rhs_scale=x_scale[:, h * SH + cols.start : h * SH + cols.stop],
                start=start,
                stop=stop,
            )

        def group_sum(dst, j, t, h):
            for d in range(D):
                product(dst, j, t, h, slice(d * VH, (d + 1) * VH), d == 0, d == D - 1)

        magnitude = [keep.tile([P, PACK, SH], F32, name="magnitude%d" % h) for h in range(HALVES)]
        pair_max = [keep.tile([P, PACK, 2 * VH], F32, name="pair_max%d" % h) for h in range(HALVES)]
        group_max = keep.tile([P, PACK, V], F32, name="group_max")
        root = keep.tile([P, PACK, V], F32, name="root")
        inverse = keep.tile([P, PACK, V], F32, name="inverse")
        y_sum_sb = keep.tile([P, SUMMED_ON_VECTOR, V], F32, name="y_sum_sb")
        y_sum_ps = sum_banks.tile([P, PACK - SUMMED_ON_VECTOR, V], F32, name="y_sum_ps")
        z_sum = [sum_banks.tile([P, PACK, VH], F32, name="z_sum%d" % h) for h in range(HALVES)]
        z_tanh = [keep.tile([P, PACK, VH], F32, name="z_tanh%d" % h) for h in range(HALVES)]
        z_term = keep.tile([P, HALVES, PACK, VH], F32, name="z_term")
        window = [keep.tile([P, 2, V], F32, name="window%d" % t) for t in range(PACK)]
        fetched = [keep.tile([P, PACK, hi - lo], BF16, name="fetched%d" % c, align_bytes=64) for c, (lo, hi) in enumerate(PIECES)]

        def values(t, h):
            y = turn_banks.tile([P, SH], F32, name="turn")
            product(y[:], 0, t, h, slice(0, SH), True, True)
            nc.scalar.activation(out=magnitude[h][:, t, :], in_=y[:], func=ACT.Abs)
            if t < SUMMED_ON_VECTOR:
                nc.vector.tensor_reduce(
                    out=y_sum_sb[:, t, h * VH : (h + 1) * VH], in_=y[:].rearrange("p (d v) -> p v d", d=D), axis=AX.X, op=ALU.add
                )

        def first_max(h, planes):
            nc.vector.tensor_tensor(
                out=pair_max[h][:, planes, :], in0=magnitude[h][:, planes, 0 : 2 * VH], in1=magnitude[h][:, planes, 2 * VH : SH], op=ALU.max
            )

        def second_max(h):
            nc.vector.tensor_tensor(
                out=group_max[:, :, h * VH : (h + 1) * VH], in0=pair_max[h][:, :, 0:VH], in1=pair_max[h][:, :, VH : 2 * VH], op=ALU.max
            )

        def zero_points(h):
            for t in range(PACK):
                group_sum(z_sum[h][:, t, :], 1, t, h)
            nc.scalar.activation(out=z_tanh[h][:], in_=z_sum[h][:], func=ACT.Tanh, scale=1.0 / D)

        def zero_term(h):
            nc.vector.tensor_tensor(out=z_term[:, h, :, :], in0=z_sum[h][:], in1=z_tanh[h][:], op=ALU.mult)

        def numerator(t):
            y_sum = y_sum_sb[:, t, :] if t < SUMMED_ON_VECTOR else y_sum_ps[:, t - SUMMED_ON_VECTOR, :]
            nc.vector.scalar_tensor_tensor(
                out=window[t][:, 1, :].rearrange("p (h v) -> p h v", h=HALVES),
                in0=y_sum.rearrange("p (h v) -> p h v", h=HALVES),
                scalar=unit_mean[:, t : t + 1],
                in1=z_term[:, :, t, :],
                op0=ALU.mult,
                op1=ALU.mult,
            )

        low_planes, high_planes, all_planes = slice(0, 2), slice(2, PACK), slice(0, PACK)
        for t in range(PACK):
            values(t, 0)
        values(0, 1)
        values(1, 1)
        zero_points(0)
        first_max(0, low_planes)
        first_max(0, high_planes)
        values(2, 1)
        values(3, 1)
        zero_points(1)
        second_max(0)
        first_max(1, all_planes)
        zero_term(0)
        second_max(1)
        zero_term(1)
        for t in range(SUMMED_ON_VECTOR, PACK):
            for h in range(HALVES):
                group_sum(y_sum_ps[:, t - SUMMED_ON_VECTOR, h * VH : (h + 1) * VH], 0, t, h)
        for t in range(PACK):
            numerator(t)

        for planes in (low_planes, high_planes):
            nc.scalar.activation(out=root[:, planes, :], in_=group_max[:, planes, :], func=ACT.Abs_reciprocal_sqrt, bias=SCALE_FLOOR)
        for planes in (low_planes, high_planes):
            nc.scalar.activation(out=inverse[:, planes, :], in_=root[:, planes, :], func=ACT.Square)

        woven = [keep.tile([P, hi - lo, PACK], BF16, name="woven%d" % c, align_bytes=64) for c, (lo, hi) in enumerate(PIECES)]
        hid_code = [keep.tile([P, hi - lo], U32, name="hid_code%d" % c, align_bytes=64) for c, (lo, hi) in enumerate(PIECES)]
        hid_scale = [keep.tile([P, hi - lo], U8, name="hid_scale%d" % c, align_bytes=64) for c, (lo, hi) in enumerate(PIECES)]

        for t in range(PACK):
            nc.vector.tensor_tensor(out=window[t][:, 0, :], in0=window[t][:, 1, :], in1=inverse[:, t, :], op=ALU.mult)

        for c, (lo, hi) in enumerate(PIECES):
            first_on_vector = PACK - 1 if c == 0 else PACK - 2
            for t in range(PACK):
                looked_up = window[t][:].rearrange("p a v -> p (a v)").indirect(rdr_sb[:, lo // LIST_ROWS : hi // LIST_ROWS])
                if t >= first_on_vector:
                    nc.vector.tensor_copy(out=fetched[c][:, t, :], in_=looked_up)
                else:
                    nc.scalar.activation(out=fetched[c][:, t, :], in_=looked_up, func=ACT.Copy)

        for c in range(len(PIECES)):
            nc.vector.tensor_copy(out=woven[c][:], in_=fetched[c][:].rearrange("p t r -> p r t"))
            nc.vector.quantize_mx(out=hid_code[c][:].bitcast(FP8X4), scales=hid_scale[c][:], in_=woven[c][:].rearrange("p r t -> p (r t)"))

        for c, (lo, hi) in enumerate(PIECES):
            acc = turn_banks.tile([P, SH], F32, name="turn")
            nc.tensor.matmul_mx(
                out=acc[:, 0 : hi - lo],
                lhsT=w3_sb[:].bitcast(FP4X4),
                lhsT_scale=w3s_sb[:],
                rhs=hid_code[c][:].bitcast(FP8X4),
                rhs_scale=hid_scale[c][:],
                start=True,
                stop=True,
            )
            result = keep.tile([P, hi - lo], F32, name="result%d" % c)
            nc.scalar.copy(out=result[:], in_=acc[:, 0 : hi - lo])
            nc.sync.dma_start(out=out[:, lo:hi], in_=result[:])
